import numpy as np
CORES = [1,9,17,25,33,41,49,57,65,73,81,89,97,105,113,121]
N = 16
def setup_inputs(rng):
    return {"x": rng.standard_normal((N, 128, 2048), dtype=np.float32)}
def reference(x):
    s = x.sum(axis=0, dtype=np.float64).astype(x.dtype)
    b = 2048 // N
    return {"y": np.stack([s[:, r * b:(r + 1) * b] for r in range(N)])}

@@ -1,0 +1,144 @@
+import concourse.bass as bass
+import concourse.mybir as mybir
+E = 2
+PB = 2
+PA = 7
+FWD = [4, 5, 6, 7]
+FA = 0
+FB = 3
+JPER = 8 // E
+SCRATCH = {'xs': ('sbuf', [128, 2048], 'float32'), 'fw': ('dram', [8, 128, 128], 'float32'), 'la': ('dram', [9, 128, 128], 'float32'), 'res': ('dram', [3, 128, 128], 'float32')}
+SEMAPHORES = ['st', 'snt', 'ra', 'rb', 'rp', 'arr'] + ['f%d' % c for c in range(8)] + ['l%d' % c for c in range(8)]
+
+def sem_f(T, c):
+    return [T.sem.f0, T.sem.f1, T.sem.f2, T.sem.f3, T.sem.f4, T.sem.f5, T.sem.f6, T.sem.f7][c]
+
+def sem_l(T, c):
+    return [T.sem.l0, T.sem.l1, T.sem.l2, T.sem.l3, T.sem.l4, T.sem.l5, T.sem.l6, T.sem.l7][c]
+
+def groups(k):
+    rot = [(k + 1 + i) % 8 for i in range(8)]
+    return [rot[c * JPER:(c + 1) * JPER] for c in range(E)]
+
+def early(s, j):
+    return j not in groups(s)[-1]
+
+def fwd_plan(k):
+    out, n = ([], 0)
+    for js in groups(k):
+        per = {}
+        for j in js:
+            if j != k:
+                per.setdefault(FWD[n % len(FWD)], []).append(j)
+                n += 1
+        out.append(per)
+    return out
+
+def fwd_engines(n):
+    e = 8
+    while e * n > 8:
+        e //= 2
+    return e
+
+def fwd_count(s, j):
+    for per in fwd_plan(s):
+        for lst in per.values():
+            if j in lst:
+                return fwd_engines(len(lst))
+    return 0
+
+def xfer(topo, dst_core, mask, sem, src, dst):
+    rid, pid, se = topo.addr(dst_core)
+    return bass.RemoteDMATransfer(dst_ids=[bass.DstId(rid=rid, pnc=pid)], dma_engine_mask=mask, remote_sem=sem, src=src, dst=dst)
+
+def fold(topo, dst_core, mask, sem, srcs, dst):
+    rid, pid, se = topo.addr(dst_core)
+    return bass.RemoteDMATransfer(dst_ids=[bass.DstId(rid=rid, pnc=pid)], dma_engine_mask=mask, remote_sem=sem, srcs=srcs, dsts=[dst], alu_op=1)
+
+def rank_core(g, T, topo, k, p):
+    base = (2 * k + p) * 8
+    gs = groups(k)
+    plan = fwd_plan(k)
+    where = {}
+    for c in range(E):
+        for f, lst in plan[c].items():
+            for j in lst:
+                where[j] = f
+
+    def load(c):
+        runs = []
+        for j in sorted(gs[c]):
+            if runs and runs[-1][1] == j:
+                runs[-1][1] = j + 1
+            else:
+                runs.append([j, j + 1])
+        for a, b in runs:
+            g.dma_start(T.xs[:, 256 * a:256 * b], T.x[:, 256 * a:256 * b]).then_inc(sem_l(T, c), 16)
+        return 16 * len(runs)
+
+    def block(b):
+        return T.xs[:, 128 * b:128 * (b + 1)]
+    loaded = [load(0)]
+    for c in range(E):
+        if c + 1 < E:
+            loaded.append(load(c + 1))
+        g.wait_ge(sem_l(T, c), loaded[c])
+        tr = []
+        for i, j in enumerate(gs[c]):
+            m = (1 << E) - 1 << i * E
+            tr.append(xfer(topo, (2 * j + p) * 8 + (PB if early(k, j) else FB), m, T.sem.arr, block(2 * j + 1 - p), T.la[k]))
+            if j == k:
+                tr.append(xfer(topo, base + FA, m << 8, T.sem.arr, block(2 * j + p), T.la[k]))
+            else:
+                tr.append(xfer(topo, base + where[j], m << 8, sem_f(T, c), block(2 * j + p), T.fw[j]))
+        g.remote_dma_fused(tr, local_sem=T.sem.snt)
+    add = mybir.AluOpType.add
+    g.wait_ge(T.sem.rp, 8)
+    g.dma_start(T.y[:], T.res[0]).then_inc(T.sem.st, 16)
+    g.wait_ge(T.sem.rb, 8)
+    g.wait_ge(T.sem.st, 16)
+    g.dma_start(T.y[:], T.res[1], accum_op=add, max_dma_last_dim=8192).then_inc(T.sem.st, 16)
+    g.wait_ge(T.sem.ra, 16)
+    g.wait_ge(T.sem.st, 32)
+    g.dma_start(T.y[:], T.res[2], accum_op=add, max_dma_last_dim=8192).then_inc(T.sem.st, 16)
+    g.wait_ge(T.sem.snt, 16 * E)
+    g.wait_ge(T.sem.st, 48)
+
+def helper_core(g, T, topo, k, p, me):
+    base = (2 * k + p) * 8
+    sent = 0
+    if me in FWD:
+        plan = fwd_plan(k)
+        for c in range(E):
+            lst = plan[c].get(me, [])
+            if not lst:
+                continue
+            g.wait_ge(sem_f(T, c), E * len(lst))
+            e = fwd_engines(len(lst))
+            tr = [xfer(topo, (2 * j + p) * 8 + (PA if early(k, j) else FA), (1 << e) - 1 << i * e, T.sem.arr, T.fw[j], T.la[k]) for i, j in enumerate(lst)]
+            g.remote_dma_fused(tr, local_sem=T.sem.snt)
+            sent += e * len(lst)
+    first = [s for s in range(8) if early(s, k)]
+    rest = [s for s in range(8) if s not in first]
+    if me == PB or me == FB:
+        srcs = first if me == PB else rest
+        g.wait_ge(T.sem.arr, E * len(srcs))
+        g.remote_dma_fused([fold(topo, (base ^ 8) + 1, 255, T.sem.rp if me == PB else T.sem.rb, [T.la[s] for s in srcs], T.res[0 if me == PB else 1])], local_sem=T.sem.snt)
+        sent += 8
+    if me == PA:
+        g.wait_ge(T.sem.arr, sum((fwd_count(s, k) for s in first)))
+        g.remote_dma_fused([fold(topo, base + FA, 65535, T.sem.arr, [T.la[s] for s in first], T.la[8])], local_sem=T.sem.snt)
+        sent += 16
+    if me == FA:
+        g.wait_ge(T.sem.arr, sum((E if s == k else fwd_count(s, k) for s in rest)) + 16)
+        g.remote_dma_fused([fold(topo, base + 1, 65535, T.sem.ra, [T.la[s] for s in rest] + [T.la[8]], T.res[2])], local_sem=T.sem.snt)
+        sent += 16
+    if sent:
+        g.wait_ge(T.sem.snt, sent)
+
+def rank_program(g, core, T, topo):
+    ch, me = (core // 8, core % 8)
+    if me == 1:
+        rank_core(g, T, topo, ch // 2, ch % 2)
+    else:
+        helper_core(g, T, topo, ch // 2, ch % 2, me)

@@ -1,144 +1,126 @@
 import concourse.bass as bass
 import concourse.mybir as mybir
-E = 2
-PB = 2
-PA = 7
-FWD = [4, 5, 6, 7]
-FA = 0
-FB = 3
-JPER = 8 // E
-SCRATCH = {'xs': ('sbuf', [128, 2048], 'float32'), 'fw': ('dram', [8, 128, 128], 'float32'), 'la': ('dram', [9, 128, 128], 'float32'), 'res': ('dram', [3, 128, 128], 'float32')}
-SEMAPHORES = ['st', 'snt', 'ra', 'rb', 'rp', 'arr'] + ['f%d' % c for c in range(8)] + ['l%d' % c for c in range(8)]
 
-def sem_f(T, c):
-    return [T.sem.f0, T.sem.f1, T.sem.f2, T.sem.f3, T.sem.f4, T.sem.f5, T.sem.f6, T.sem.f7][c]
+CH = [[0, 1, 2, 3], [4, 5, 6, 7]]
+MC = [2, 6, 3, 7]
+QA, QB = 4, 0
+EARLY = [0, 1, 2, 3]
 
-def sem_l(T, c):
-    return [T.sem.l0, T.sem.l1, T.sem.l2, T.sem.l3, T.sem.l4, T.sem.l5, T.sem.l6, T.sem.l7][c]
+SCRATCH = {
+    'xs': ('sbuf', [128, 2048], 'float32'),
+    'mr': ('sbuf', [128, 1024], 'float32'),
+    'qa': ('dram', [9, 128, 128], 'float32'),
+    'res': ('dram', [1, 128, 128], 'float32'),
+}
+SEMAPHORES = (['snt', 'arr', 'fin', 'st'] + ['ld%d' % t for t in range(8)]
+              + ['a0', 'a1', 'b0', 'b1'])
 
-def groups(k):
-    rot = [(k + 1 + i) % 8 for i in range(8)]
-    return [rot[c * JPER:(c + 1) * JPER] for c in range(E)]
 
-def early(s, j):
-    return j not in groups(s)[-1]
+def sem(T, name):
+    return {'ld0': T.sem.ld0, 'ld1': T.sem.ld1, 'ld2': T.sem.ld2, 'ld3': T.sem.ld3,
+            'ld4': T.sem.ld4, 'ld5': T.sem.ld5, 'ld6': T.sem.ld6, 'ld7': T.sem.ld7,
+            'a0': T.sem.a0, 'a1': T.sem.a1, 'b0': T.sem.b0, 'b1': T.sem.b1}[name]
 
-def fwd_plan(k):
-    out, n = ([], 0)
-    for js in groups(k):
-        per = {}
-        for j in js:
-            if j != k:
-                per.setdefault(FWD[n % len(FWD)], []).append(j)
-                n += 1
-        out.append(per)
-    return out
 
-def fwd_engines(n):
-    e = 8
-    while e * n > 8:
-        e //= 2
-    return e
+def engines_of(i):
+    for c in CH:
+        if i in c:
+            return 16 // len(c)
 
-def fwd_count(s, j):
-    for per in fwd_plan(s):
-        for lst in per.values():
-            if j in lst:
-                return fwd_engines(len(lst))
-    return 0
 
-def xfer(topo, dst_core, mask, sem, src, dst):
+def xfer(topo, dst_core, mask, s, src, dst):
     rid, pid, se = topo.addr(dst_core)
-    return bass.RemoteDMATransfer(dst_ids=[bass.DstId(rid=rid, pnc=pid)], dma_engine_mask=mask, remote_sem=sem, src=src, dst=dst)
+    return bass.RemoteDMATransfer(dst_ids=[bass.DstId(rid=rid, pnc=pid)], dma_engine_mask=mask,
+                                  remote_sem=s, src=src, dst=dst)
 
-def fold(topo, dst_core, mask, sem, srcs, dst):
+
+def fold(topo, dst_core, mask, s, srcs, dst):
     rid, pid, se = topo.addr(dst_core)
-    return bass.RemoteDMATransfer(dst_ids=[bass.DstId(rid=rid, pnc=pid)], dma_engine_mask=mask, remote_sem=sem, srcs=srcs, dsts=[dst], alu_op=1)
+    return bass.RemoteDMATransfer(dst_ids=[bass.DstId(rid=rid, pnc=pid)], dma_engine_mask=mask,
+                                  remote_sem=s, srcs=srcs, dsts=[dst], alu_op=1)
+
+
+def ranges(js):
+    runs = []
+    for j in sorted(js):
+        if runs and runs[-1][1] == 256 * j:
+            runs[-1][1] = 256 * (j + 1)
+        else:
+            runs.append([256 * j, 256 * (j + 1)])
+    if len(runs) == 1:
+        a, b = runs[0]
+        m = (a + b) // 2
+        runs = [[a, m], [m, b]]
+    return runs
+
 
 def rank_core(g, T, topo, k, p):
     base = (2 * k + p) * 8
-    gs = groups(k)
-    plan = fwd_plan(k)
-    where = {}
-    for c in range(E):
-        for f, lst in plan[c].items():
-            for j in lst:
-                where[j] = f
-
-    def load(c):
-        runs = []
-        for j in sorted(gs[c]):
-            if runs and runs[-1][1] == j:
-                runs[-1][1] = j + 1
-            else:
-                runs.append([j, j + 1])
-        for a, b in runs:
-            g.dma_start(T.xs[:, 256 * a:256 * b], T.x[:, 256 * a:256 * b]).then_inc(sem_l(T, c), 16)
-        return 16 * len(runs)
-
-    def block(b):
-        return T.xs[:, 128 * b:128 * (b + 1)]
-    loaded = [load(0)]
-    for c in range(E):
-        if c + 1 < E:
-            loaded.append(load(c + 1))
-        g.wait_ge(sem_l(T, c), loaded[c])
+    nld = []
+    for c, pos in enumerate(CH):
+        rs = ranges([(k + i) % 8 for i in pos])
+        for n, (a, b) in enumerate(rs):
+            q = g.sync if n % 2 == 0 else g.scalar
+            q.dma_start(T.xs[:, a:b], T.x[:, a:b]).then_inc(sem(T, 'ld%d' % c), 16)
+        nld.append(16 * len(rs))
+    for c, pos in enumerate(CH):
+        e = 16 // len(pos)
+        g.wait_ge(sem(T, 'ld%d' % c), nld[c])
         tr = []
-        for i, j in enumerate(gs[c]):
-            m = (1 << E) - 1 << i * E
-            tr.append(xfer(topo, (2 * j + p) * 8 + (PB if early(k, j) else FB), m, T.sem.arr, block(2 * j + 1 - p), T.la[k]))
-            if j == k:
-                tr.append(xfer(topo, base + FA, m << 8, T.sem.arr, block(2 * j + p), T.la[k]))
-            else:
-                tr.append(xfer(topo, base + where[j], m << 8, sem_f(T, c), block(2 * j + p), T.fw[j]))
+        for n, i in enumerate(pos):
+            j = (k + i) % 8
+            tr.append(xfer(topo, base + MC[i % 4], ((1 << e) - 1) << (n * e), sem(T, 'a%d' % (i // 4)),
+                           T.xs[:, 256 * j:256 * (j + 1)], T.xs[:, 256 * j:256 * (j + 1)]))
         g.remote_dma_fused(tr, local_sem=T.sem.snt)
-    add = mybir.AluOpType.add
-    g.wait_ge(T.sem.rp, 8)
-    g.dma_start(T.y[:], T.res[0]).then_inc(T.sem.st, 16)
-    g.wait_ge(T.sem.rb, 8)
+    g.sync.wait_ge(T.sem.fin, 16)
+    g.sync.dma_start(T.y[:], T.res[0]).then_inc(T.sem.st, 16)
+    g.wait_ge(T.sem.snt, 16 * len(CH))
     g.wait_ge(T.sem.st, 16)
-    g.dma_start(T.y[:], T.res[1], accum_op=add, max_dma_last_dim=8192).then_inc(T.sem.st, 16)
-    g.wait_ge(T.sem.ra, 16)
-    g.wait_ge(T.sem.st, 32)
-    g.dma_start(T.y[:], T.res[2], accum_op=add, max_dma_last_dim=8192).then_inc(T.sem.st, 16)
-    g.wait_ge(T.sem.snt, 16 * E)
-    g.wait_ge(T.sem.st, 48)
 
-def helper_core(g, T, topo, k, p, me):
+
+def mate_core(g, T, topo, k, p, me):
     base = (2 * k + p) * 8
-    sent = 0
-    if me in FWD:
-        plan = fwd_plan(k)
-        for c in range(E):
-            lst = plan[c].get(me, [])
-            if not lst:
-                continue
-            g.wait_ge(sem_f(T, c), E * len(lst))
-            e = fwd_engines(len(lst))
-            tr = [xfer(topo, (2 * j + p) * 8 + (PA if early(k, j) else FA), (1 << e) - 1 << i * e, T.sem.arr, T.fw[j], T.la[k]) for i, j in enumerate(lst)]
-            g.remote_dma_fused(tr, local_sem=T.sem.snt)
-            sent += e * len(lst)
-    first = [s for s in range(8) if early(s, k)]
+    mi = MC.index(me)
+
+    def blk(b):
+        return T.xs[:, 128 * b:128 * (b + 1)]
+
+    for u in range(2):
+        i = mi + 4 * u
+        j = (k + i) % 8
+        got = T.mr[:, 128 * j:128 * (j + 1)]
+        g.wait_ge(sem(T, 'a%d' % u), engines_of(i))
+        g.remote_dma_fused([xfer(topo, (base ^ 8) + me, 0xFF, sem(T, 'b%d' % u), blk(2 * j + 1 - p), got)],
+                           local_sem=T.sem.snt)
+        g.wait_ge(sem(T, 'b%d' % u), 8)
+        g.remote_dma_fused([fold(topo, (2 * j + p) * 8 + (QA if i in EARLY else QB), 0xFF, T.sem.arr,
+                                 [blk(2 * j + p), got], T.qa[k])], local_sem=T.sem.snt)
+    g.wait_ge(T.sem.snt, 32)
+
+
+def fold_core(g, T, topo, k, p, me):
+    base = (2 * k + p) * 8
+    first = [s for s in range(8) if (k - s) % 8 in EARLY]
     rest = [s for s in range(8) if s not in first]
-    if me == PB or me == FB:
-        srcs = first if me == PB else rest
-        g.wait_ge(T.sem.arr, E * len(srcs))
-        g.remote_dma_fused([fold(topo, (base ^ 8) + 1, 255, T.sem.rp if me == PB else T.sem.rb, [T.la[s] for s in srcs], T.res[0 if me == PB else 1])], local_sem=T.sem.snt)
-        sent += 8
-    if me == PA:
-        g.wait_ge(T.sem.arr, sum((fwd_count(s, k) for s in first)))
-        g.remote_dma_fused([fold(topo, base + FA, 65535, T.sem.arr, [T.la[s] for s in first], T.la[8])], local_sem=T.sem.snt)
-        sent += 16
-    if me == FA:
-        g.wait_ge(T.sem.arr, sum((E if s == k else fwd_count(s, k) for s in rest)) + 16)
-        g.remote_dma_fused([fold(topo, base + 1, 65535, T.sem.ra, [T.la[s] for s in rest] + [T.la[8]], T.res[2])], local_sem=T.sem.snt)
-        sent += 16
-    if sent:
-        g.wait_ge(T.sem.snt, sent)
+    if me == QA and first:
+        g.wait_ge(T.sem.arr, 8 * len(first))
+        g.remote_dma_fused([fold(topo, base + QB, 0xFFFF, T.sem.arr, [T.qa[s] for s in first], T.qa[8])],
+                           local_sem=T.sem.snt)
+        g.wait_ge(T.sem.snt, 16)
+    if me == QB:
+        g.wait_ge(T.sem.arr, 8 * len(rest) + (16 if first else 0))
+        g.remote_dma_fused([fold(topo, base + 1, 0xFFFF, T.sem.fin,
+                                 [T.qa[s] for s in rest] + ([T.qa[8]] if first else []), T.res[0])],
+                           local_sem=T.sem.snt)
+        g.wait_ge(T.sem.snt, 16)
+
 
 def rank_program(g, core, T, topo):
-    ch, me = (core // 8, core % 8)
+    ch, me = core // 8, core % 8
+    k, p = ch // 2, ch % 2
     if me == 1:
-        rank_core(g, T, topo, ch // 2, ch % 2)
-    else:
-        helper_core(g, T, topo, ch // 2, ch % 2, me)
+        rank_core(g, T, topo, k, p)
+    elif me in MC:
+        mate_core(g, T, topo, k, p, me)
+    elif me in (QA, QB):
+        fold_core(g, T, topo, k, p, me)

@@ -4,13 +4,14 @@ import concourse.mybir as mybir
 CH = [[0, 1, 2, 3], [4, 5, 6, 7]]
 MC = [2, 6, 3, 7]
 QA, QB = 4, 0
-EARLY = [0, 1, 2, 3]
+EARLY = []
+QSB = False
 
 SCRATCH = {
     'xs': ('sbuf', [128, 2048], 'float32'),
     'mr': ('sbuf', [128, 1024], 'float32'),
-    'qa': ('dram', [9, 128, 128], 'float32'),
-    'res': ('dram', [1, 128, 128], 'float32'),
+    'qa': ('sbuf', [128, 9 * 128], 'float32') if QSB else ('dram', [9, 128, 128], 'float32'),
+    'res': ('sbuf', [128, 128], 'float32') if QSB else ('dram', [1, 128, 128], 'float32'),
 }
 SEMAPHORES = (['snt', 'arr', 'fin', 'st'] + ['ld%d' % t for t in range(8)]
               + ['a0', 'a1', 'b0', 'b1'])
@@ -20,6 +21,14 @@ def sem(T, name):
     return {'ld0': T.sem.ld0, 'ld1': T.sem.ld1, 'ld2': T.sem.ld2, 'ld3': T.sem.ld3,
             'ld4': T.sem.ld4, 'ld5': T.sem.ld5, 'ld6': T.sem.ld6, 'ld7': T.sem.ld7,
             'a0': T.sem.a0, 'a1': T.sem.a1, 'b0': T.sem.b0, 'b1': T.sem.b1}[name]
+
+
+def qslot(T, s):
+    return T.qa[:, 128 * s:128 * (s + 1)] if QSB else T.qa[s]
+
+
+def rslot(T):
+    return T.res[:, :] if QSB else T.res[0]
 
 
 def engines_of(i):
@@ -73,7 +82,7 @@ def rank_core(g, T, topo, k, p):
                            T.xs[:, 256 * j:256 * (j + 1)], T.xs[:, 256 * j:256 * (j + 1)]))
         g.remote_dma_fused(tr, local_sem=T.sem.snt)
     g.sync.wait_ge(T.sem.fin, 16)
-    g.sync.dma_start(T.y[:], T.res[0]).then_inc(T.sem.st, 16)
+    g.sync.dma_start(T.y[:], rslot(T)).then_inc(T.sem.st, 16)
     g.wait_ge(T.sem.snt, 16 * len(CH))
     g.wait_ge(T.sem.st, 16)
 
@@ -86,15 +95,17 @@ def mate_core(g, T, topo, k, p, me):
         return T.xs[:, 128 * b:128 * (b + 1)]
 
     for u in range(2):
+        j = (k + mi + 4 * u) % 8
+        g.wait_ge(sem(T, 'a%d' % u), engines_of(mi + 4 * u))
+        g.remote_dma_fused([xfer(topo, (base ^ 8) + me, 0xFF, sem(T, 'b%d' % u), blk(2 * j + 1 - p),
+                                 T.mr[:, 128 * j:128 * (j + 1)])], local_sem=T.sem.snt)
+    for u in range(2):
         i = mi + 4 * u
         j = (k + i) % 8
-        got = T.mr[:, 128 * j:128 * (j + 1)]
-        g.wait_ge(sem(T, 'a%d' % u), engines_of(i))
-        g.remote_dma_fused([xfer(topo, (base ^ 8) + me, 0xFF, sem(T, 'b%d' % u), blk(2 * j + 1 - p), got)],
-                           local_sem=T.sem.snt)
         g.wait_ge(sem(T, 'b%d' % u), 8)
         g.remote_dma_fused([fold(topo, (2 * j + p) * 8 + (QA if i in EARLY else QB), 0xFF, T.sem.arr,
-                                 [blk(2 * j + p), got], T.qa[k])], local_sem=T.sem.snt)
+                                 [blk(2 * j + p), T.mr[:, 128 * j:128 * (j + 1)]], qslot(T, k))],
+                           local_sem=T.sem.snt)
     g.wait_ge(T.sem.snt, 32)
 
 
@@ -104,13 +115,13 @@ def fold_core(g, T, topo, k, p, me):
     rest = [s for s in range(8) if s not in first]
     if me == QA and first:
         g.wait_ge(T.sem.arr, 8 * len(first))
-        g.remote_dma_fused([fold(topo, base + QB, 0xFFFF, T.sem.arr, [T.qa[s] for s in first], T.qa[8])],
+        g.remote_dma_fused([fold(topo, base + QB, 0xFFFF, T.sem.arr, [qslot(T, s) for s in first], qslot(T, 8))],
                            local_sem=T.sem.snt)
         g.wait_ge(T.sem.snt, 16)
     if me == QB:
         g.wait_ge(T.sem.arr, 8 * len(rest) + (16 if first else 0))
         g.remote_dma_fused([fold(topo, base + 1, 0xFFFF, T.sem.fin,
-                                 [T.qa[s] for s in rest] + ([T.qa[8]] if first else []), T.res[0])],
+                                 [qslot(T, s) for s in rest] + ([qslot(T, 8)] if first else []), rslot(T))],
                            local_sem=T.sem.snt)
         g.wait_ge(T.sem.snt, 16)
 

@@ -3,38 +3,20 @@ import concourse.mybir as mybir
 
 CH = [[0, 1, 2, 3], [4, 5, 6, 7]]
 MC = [2, 6, 3, 7]
-QA, QB = 4, 0
-EARLY = []
-QSB = False
+QB = 0
 
 SCRATCH = {
     'xs': ('sbuf', [128, 2048], 'float32'),
     'mr': ('sbuf', [128, 1024], 'float32'),
-    'qa': ('sbuf', [128, 9 * 128], 'float32') if QSB else ('dram', [9, 128, 128], 'float32'),
-    'res': ('sbuf', [128, 128], 'float32') if QSB else ('dram', [1, 128, 128], 'float32'),
+    'qa': ('dram', [8, 128, 128], 'float32'),
+    'res': ('dram', [1, 128, 128], 'float32'),
 }
-SEMAPHORES = (['snt', 'arr', 'fin', 'st'] + ['ld%d' % t for t in range(8)]
-              + ['a0', 'a1', 'b0', 'b1'])
+SEMAPHORES = ['snt', 'arr', 'fin', 'st', 'ld0', 'ld1', 'a0', 'a1', 'b0', 'b1', 'o0', 'o1']
 
 
 def sem(T, name):
-    return {'ld0': T.sem.ld0, 'ld1': T.sem.ld1, 'ld2': T.sem.ld2, 'ld3': T.sem.ld3,
-            'ld4': T.sem.ld4, 'ld5': T.sem.ld5, 'ld6': T.sem.ld6, 'ld7': T.sem.ld7,
-            'a0': T.sem.a0, 'a1': T.sem.a1, 'b0': T.sem.b0, 'b1': T.sem.b1}[name]
-
-
-def qslot(T, s):
-    return T.qa[:, 128 * s:128 * (s + 1)] if QSB else T.qa[s]
-
-
-def rslot(T):
-    return T.res[:, :] if QSB else T.res[0]
-
-
-def engines_of(i):
-    for c in CH:
-        if i in c:
-            return 16 // len(c)
+    return {'ld0': T.sem.ld0, 'ld1': T.sem.ld1, 'a0': T.sem.a0, 'a1': T.sem.a1,
+            'b0': T.sem.b0, 'b1': T.sem.b1, 'o0': T.sem.o0, 'o1': T.sem.o1}[name]
 
 
 def xfer(topo, dst_core, mask, s, src, dst):
@@ -72,18 +54,23 @@ def rank_core(g, T, topo, k, p):
             q = g.sync if n % 2 == 0 else g.scalar
             q.dma_start(T.xs[:, a:b], T.x[:, a:b]).then_inc(sem(T, 'ld%d' % c), 16)
         nld.append(16 * len(rs))
-    for c, pos in enumerate(CH):
-        e = 16 // len(pos)
-        g.wait_ge(sem(T, 'ld%d' % c), nld[c])
+
+    def hand(c, par, name):
         tr = []
-        for n, i in enumerate(pos):
-            j = (k + i) % 8
-            tr.append(xfer(topo, base + MC[i % 4], ((1 << e) - 1) << (n * e), sem(T, 'a%d' % (i // 4)),
-                           T.xs[:, 256 * j:256 * (j + 1)], T.xs[:, 256 * j:256 * (j + 1)]))
+        for n, i in enumerate(CH[c]):
+            b = 2 * ((k + i) % 8) + par
+            tr.append(xfer(topo, base + MC[i % 4], 0xF << (4 * n), sem(T, name % c),
+                           T.xs[:, 128 * b:128 * (b + 1)], T.xs[:, 128 * b:128 * (b + 1)]))
         g.remote_dma_fused(tr, local_sem=T.sem.snt)
+
+    for c in range(2):
+        g.wait_ge(sem(T, 'ld%d' % c), nld[c])
+        hand(c, 1 - p, 'a%d')
+    for c in range(2):
+        hand(c, p, 'o%d')
     g.sync.wait_ge(T.sem.fin, 16)
-    g.sync.dma_start(T.y[:], rslot(T)).then_inc(T.sem.st, 16)
-    g.wait_ge(T.sem.snt, 16 * len(CH))
+    g.sync.dma_start(T.y[:], T.res[0]).then_inc(T.sem.st, 16)
+    g.wait_ge(T.sem.snt, 64)
     g.wait_ge(T.sem.st, 16)
 
 
@@ -96,34 +83,25 @@ def mate_core(g, T, topo, k, p, me):
 
     for u in range(2):
         j = (k + mi + 4 * u) % 8
-        g.wait_ge(sem(T, 'a%d' % u), engines_of(mi + 4 * u))
+        g.wait_ge(sem(T, 'a%d' % u), 4)
         g.remote_dma_fused([xfer(topo, (base ^ 8) + me, 0xFF, sem(T, 'b%d' % u), blk(2 * j + 1 - p),
                                  T.mr[:, 128 * j:128 * (j + 1)])], local_sem=T.sem.snt)
     for u in range(2):
-        i = mi + 4 * u
-        j = (k + i) % 8
+        j = (k + mi + 4 * u) % 8
         g.wait_ge(sem(T, 'b%d' % u), 8)
-        g.remote_dma_fused([fold(topo, (2 * j + p) * 8 + (QA if i in EARLY else QB), 0xFF, T.sem.arr,
-                                 [blk(2 * j + p), T.mr[:, 128 * j:128 * (j + 1)]], qslot(T, k))],
+        g.wait_ge(sem(T, 'o%d' % u), 4)
+        g.remote_dma_fused([fold(topo, (2 * j + p) * 8 + QB, 0xFF, T.sem.arr,
+                                 [blk(2 * j + p), T.mr[:, 128 * j:128 * (j + 1)]], T.qa[k])],
                            local_sem=T.sem.snt)
     g.wait_ge(T.sem.snt, 32)
 
 
-def fold_core(g, T, topo, k, p, me):
+def fold_core(g, T, topo, k, p):
     base = (2 * k + p) * 8
-    first = [s for s in range(8) if (k - s) % 8 in EARLY]
-    rest = [s for s in range(8) if s not in first]
-    if me == QA and first:
-        g.wait_ge(T.sem.arr, 8 * len(first))
-        g.remote_dma_fused([fold(topo, base + QB, 0xFFFF, T.sem.arr, [qslot(T, s) for s in first], qslot(T, 8))],
-                           local_sem=T.sem.snt)
-        g.wait_ge(T.sem.snt, 16)
-    if me == QB:
-        g.wait_ge(T.sem.arr, 8 * len(rest) + (16 if first else 0))
-        g.remote_dma_fused([fold(topo, base + 1, 0xFFFF, T.sem.fin,
-                                 [qslot(T, s) for s in rest] + ([qslot(T, 8)] if first else []), rslot(T))],
-                           local_sem=T.sem.snt)
-        g.wait_ge(T.sem.snt, 16)
+    g.wait_ge(T.sem.arr, 64)
+    g.remote_dma_fused([fold(topo, base + 1, 0xFFFF, T.sem.fin, [T.qa[s] for s in range(8)], T.res[0])],
+                       local_sem=T.sem.snt)
+    g.wait_ge(T.sem.snt, 16)
 
 
 def rank_program(g, core, T, topo):
@@ -133,5 +111,5 @@ def rank_program(g, core, T, topo):
         rank_core(g, T, topo, k, p)
     elif me in MC:
         mate_core(g, T, topo, k, p, me)
-    elif me in (QA, QB):
-        fold_core(g, T, topo, k, p, me)
+    elif me == QB:
+        fold_core(g, T, topo, k, p)

import concourse.bass as bass
import concourse.mybir as mybir

CH = [[0, 1, 2, 3], [4, 5, 6, 7]]
MC = [2, 6, 3, 7]
QB = 0

SCRATCH = {
    'xs': ('sbuf', [128, 2048], 'float32'),
    'mr': ('sbuf', [128, 1024], 'float32'),
    'qa': ('dram', [8, 128, 128], 'float32'),
    'res': ('dram', [1, 128, 128], 'float32'),
}
SEMAPHORES = ['snt', 'arr', 'fin', 'st', 'ld0', 'ld1', 'a0', 'a1', 'b0', 'b1', 'o0', 'o1']


def sem(T, name):
    return {'ld0': T.sem.ld0, 'ld1': T.sem.ld1, 'a0': T.sem.a0, 'a1': T.sem.a1,
            'b0': T.sem.b0, 'b1': T.sem.b1, 'o0': T.sem.o0, 'o1': T.sem.o1}[name]


def xfer(topo, dst_core, mask, s, src, dst):
    rid, pid, se = topo.addr(dst_core)
    return bass.RemoteDMATransfer(dst_ids=[bass.DstId(rid=rid, pnc=pid)], dma_engine_mask=mask,
                                  remote_sem=s, src=src, dst=dst)


def fold(topo, dst_core, mask, s, srcs, dst):
    rid, pid, se = topo.addr(dst_core)
    return bass.RemoteDMATransfer(dst_ids=[bass.DstId(rid=rid, pnc=pid)], dma_engine_mask=mask,
                                  remote_sem=s, srcs=srcs, dsts=[dst], alu_op=1)


def ranges(js):
    runs = []
    for j in sorted(js):
        if runs and runs[-1][1] == 256 * j:
            runs[-1][1] = 256 * (j + 1)
        else:
            runs.append([256 * j, 256 * (j + 1)])
    if len(runs) == 1:
        a, b = runs[0]
        m = (a + b) // 2
        runs = [[a, m], [m, b]]
    return runs


def rank_core(g, T, topo, k, p):
    base = (2 * k + p) * 8
    nld = []
    for c, pos in enumerate(CH):
        rs = ranges([(k + i) % 8 for i in pos])
        for n, (a, b) in enumerate(rs):
            q = g.sync if n % 2 == 0 else g.scalar
            q.dma_start(T.xs[:, a:b], T.x[:, a:b]).then_inc(sem(T, 'ld%d' % c), 16)
        nld.append(16 * len(rs))

    def hand(c, par, name):
        tr = []
        for n, i in enumerate(CH[c]):
            b = 2 * ((k + i) % 8) + par
            tr.append(xfer(topo, base + MC[i % 4], 0xF << (4 * n), sem(T, name % c),
                           T.xs[:, 128 * b:128 * (b + 1)], T.xs[:, 128 * b:128 * (b + 1)]))
        g.remote_dma_fused(tr, local_sem=T.sem.snt)

    for c in range(2):
        g.wait_ge(sem(T, 'ld%d' % c), nld[c])
        hand(c, 1 - p, 'a%d')
    for c in range(2):
        hand(c, p, 'o%d')
    g.sync.wait_ge(T.sem.fin, 16)
    g.sync.dma_start(T.y[:], T.res[0]).then_inc(T.sem.st, 16)
    g.wait_ge(T.sem.snt, 64)
    g.wait_ge(T.sem.st, 16)


def mate_core(g, T, topo, k, p, me):
    base = (2 * k + p) * 8
    mi = MC.index(me)

    def blk(b):
        return T.xs[:, 128 * b:128 * (b + 1)]

    for u in range(2):
        j = (k + mi + 4 * u) % 8
        g.wait_ge(sem(T, 'a%d' % u), 4)
        g.remote_dma_fused([xfer(topo, (base ^ 8) + me, 0xFF, sem(T, 'b%d' % u), blk(2 * j + 1 - p),
                                 T.mr[:, 128 * j:128 * (j + 1)])], local_sem=T.sem.snt)
    for u in range(2):
        j = (k + mi + 4 * u) % 8
        g.wait_ge(sem(T, 'b%d' % u), 8)
        g.wait_ge(sem(T, 'o%d' % u), 4)
        g.remote_dma_fused([fold(topo, (2 * j + p) * 8 + QB, 0xFF, T.sem.arr,
                                 [blk(2 * j + p), T.mr[:, 128 * j:128 * (j + 1)]], T.qa[k])],
                           local_sem=T.sem.snt)
    g.wait_ge(T.sem.snt, 32)


def fold_core(g, T, topo, k, p):
    base = (2 * k + p) * 8
    g.wait_ge(T.sem.arr, 64)
    g.remote_dma_fused([fold(topo, base + 1, 0xFFFF, T.sem.fin, [T.qa[s] for s in range(8)], T.res[0])],
                       local_sem=T.sem.snt)
    g.wait_ge(T.sem.snt, 16)


def rank_program(g, core, T, topo):
    ch, me = core // 8, core % 8
    k, p = ch // 2, ch % 2
    if me == 1:
        rank_core(g, T, topo, k, p)
    elif me in MC:
        mate_core(g, T, topo, k, p, me)
    elif me == QB:
        fold_core(g, T, topo, k, p)
